import numpy as np, ml_dtypes
CORES = [32,33,34,35,36,37,38,39,40,41,42,43,44,45,46,47,48,49,50,51,52,53,54,55,56,57,58,59,60,61,62,63]
N = 32
def setup_inputs(rng):
    return {"x": rng.standard_normal((N, 128, 2048), dtype=np.float32).astype(ml_dtypes.bfloat16)}
def reference(x):
    s = x.sum(axis=0, dtype=np.float64).astype(x.dtype)
    b = 2048 // N
    return {"y": np.stack([s[:, r * b:(r + 1) * b] for r in range(N)])}

@@ -1,0 +1,84 @@
+from concourse.bass import DstId, RemoteDMATransfer
+
+SCRATCH = {
+    "xd": ("dram", [32, 128, 64], "bfloat16"),
+    "land1": ("dram", [32, 128, 64], "bfloat16"),
+    "land2": ("dram", [4, 128, 64], "bfloat16"),
+    "grp": ("dram", [4, 128, 64], "bfloat16"),
+}
+SEMAPHORES = ["ldA", "ldB", "sent", "arr1", "arr2", "arr3", "stored"]
+
+FIRST_CHIP = 4
+
+
+def reducer_of(c, m):
+    cc, hi = FIRST_CHIP + m // 2, m % 2
+    if cc == c:
+        return 5 if hi else 1
+    if cc == c ^ 2:
+        return 0 if hi else 4
+    if cc == c ^ 1:
+        return 2 if hi else 6
+    return 3 if hi else 7
+
+
+def rank_program(g, core, T, topo):
+    rank = T.rank_of(core)
+    if rank is None:
+        return
+    c, k = topo.chip(core), core % 8
+    sem = T.sem
+
+    def dst(cr):
+        rid, pid, _se = topo.addr(cr)
+        return DstId(rid=rid, pnc=pid)
+
+    my_group = [m for m in range(8) if reducer_of(c, m) == k][0]
+    first = [m for m in range(8) if reducer_of(c, m) in (2, 3, 6, 7)]
+    second = [m for m in range(8) if reducer_of(c, m) not in (2, 3, 6, 7)]
+
+    for groups, ld in ((first, sem.ldA), (second, sem.ldB)):
+        for i, m in enumerate(groups):
+            q = g.sync if i % 2 == 0 else g.scalar
+            q.dma_start(T.xd[4 * m:4 * m + 4], T.x[:, 256 * m:256 * m + 256]).then_inc(ld, 16)
+
+    sent = 0
+    for groups, ld in ((first, sem.ldA), (second, sem.ldB)):
+        g.wait_ge(ld, 64)
+        trs = []
+        for m in groups:
+            if m == my_group:
+                continue
+            d = dst(8 * c + reducer_of(c, m))
+            for q in range(4):
+                trs.append(RemoteDMATransfer(dst_ids=[d], dma_engine_mask=1 << len(trs), remote_sem=sem.arr1,
+                                             src=T.xd[4 * m + q], dst=T.land1[4 * k + q], alu_op=0))
+        g.remote_dma_fused(trs, local_sem=sem.sent)
+        sent += len(trs)
+
+    g.wait_ge(sem.arr1, 28)
+    cc, hi = FIRST_CHIP + my_group // 2, my_group % 2
+    ne = 4 if cc == c else 2
+    trs = []
+    for q in range(4):
+        coll = 8 * cc + (q if hi else 4 + q)
+        srcs = [T.land1[4 * j + q] for j in range(8) if j != k] + [T.xd[4 * my_group + q]]
+        trs.append(RemoteDMATransfer(dst_ids=[dst(coll)], dma_engine_mask=((1 << ne) - 1) << (ne * q),
+                                     remote_sem=sem.arr2, srcs=srcs, dsts=[T.land2[c - FIRST_CHIP]], alu_op=1))
+    g.remote_dma_fused(trs, local_sem=sem.sent)
+    sent += 4 * ne
+
+    g.wait_ge(sem.arr2, 2 + 2 + 2 + 4)
+    q = k % 4
+    owners = [8 * c + (4 + t if k < 4 else t) for t in range(4)]
+    g.remote_dma_fused([RemoteDMATransfer(dst_ids=[dst(o) for o in owners], dma_engine_mask=0xFFFF,
+                                          remote_sem=sem.arr3, srcs=[T.land2[i] for i in range(4)],
+                                          dsts=[T.grp[q] for _o in owners], alu_op=1)], local_sem=sem.sent)
+    sent += 16
+
+    t = k % 4
+    g.sync.wait_ge(sem.arr3, 64)
+    g.sync.dma_start(T.y[:], T.grp[:, t::4, :]).then_inc(sem.stored, 16)
+
+    g.wait_ge(sem.sent, sent)
+    g.wait_ge(sem.stored, 16)

@@ -11,15 +11,20 @@ SEMAPHORES = ["ldA", "ldB", "sent", "arr1", "arr2", "arr3", "stored"]
 FIRST_CHIP = 4
 
 
-def reducer_of(c, m):
+def reducer_of(c, m, q):
     cc, hi = FIRST_CHIP + m // 2, m % 2
     if cc == c:
-        return 5 if hi else 1
+        return (4 if hi else 0) + q // 2
     if cc == c ^ 2:
-        return 0 if hi else 4
+        return (0 if hi else 4) + q // 2
     if cc == c ^ 1:
         return 2 if hi else 6
     return 3 if hi else 7
+
+
+def units_of(c, k):
+    us = [(m, q) for m in range(8) for q in range(4) if reducer_of(c, m, q) == k]
+    return sorted(us, key=lambda u: (FIRST_CHIP + u[0] // 2 == c, u))
 
 
 def rank_program(g, core, T, topo):
@@ -33,42 +38,43 @@ def rank_program(g, core, T, topo):
         rid, pid, _se = topo.addr(cr)
         return DstId(rid=rid, pnc=pid)
 
-    my_group = [m for m in range(8) if reducer_of(c, m) == k][0]
-    first = [m for m in range(8) if reducer_of(c, m) in (2, 3, 6, 7)]
-    second = [m for m in range(8) if reducer_of(c, m) not in (2, 3, 6, 7)]
+    mine = units_of(c, k)
+    first = [m for m in range(8) if (FIRST_CHIP + m // 2 - c) % 2 == 1]
+    second = [m for m in range(8) if m not in first]
 
     for groups, ld in ((first, sem.ldA), (second, sem.ldB)):
         for i, m in enumerate(groups):
-            q = g.sync if i % 2 == 0 else g.scalar
-            q.dma_start(T.xd[4 * m:4 * m + 4], T.x[:, 256 * m:256 * m + 256]).then_inc(ld, 16)
+            qu = g.sync if i % 2 == 0 else g.scalar
+            qu.dma_start(T.xd[4 * m:4 * m + 4], T.x[:, 256 * m:256 * m + 256]).then_inc(ld, 16)
 
     sent = 0
     for groups, ld in ((first, sem.ldA), (second, sem.ldB)):
         g.wait_ge(ld, 64)
         trs = []
         for m in groups:
-            if m == my_group:
-                continue
-            d = dst(8 * c + reducer_of(c, m))
             for q in range(4):
-                trs.append(RemoteDMATransfer(dst_ids=[d], dma_engine_mask=1 << len(trs), remote_sem=sem.arr1,
-                                             src=T.xd[4 * m + q], dst=T.land1[4 * k + q], alu_op=0))
+                r = reducer_of(c, m, q)
+                if r == k:
+                    continue
+                u = units_of(c, r).index((m, q))
+                trs.append(RemoteDMATransfer(dst_ids=[dst(8 * c + r)], dma_engine_mask=1 << len(trs),
+                                             remote_sem=sem.arr1, src=T.xd[4 * m + q], dst=T.land1[4 * k + u],
+                                             alu_op=0))
         g.remote_dma_fused(trs, local_sem=sem.sent)
         sent += len(trs)
 
     g.wait_ge(sem.arr1, 28)
-    cc, hi = FIRST_CHIP + my_group // 2, my_group % 2
-    ne = 4 if cc == c else 2
+    ne = 2 if k in (2, 3, 6, 7) else 4
     trs = []
-    for q in range(4):
-        coll = 8 * cc + (q if hi else 4 + q)
-        srcs = [T.land1[4 * j + q] for j in range(8) if j != k] + [T.xd[4 * my_group + q]]
-        trs.append(RemoteDMATransfer(dst_ids=[dst(coll)], dma_engine_mask=((1 << ne) - 1) << (ne * q),
+    for u, (m, q) in enumerate(mine):
+        coll = 8 * (FIRST_CHIP + m // 2) + (q if m % 2 else 4 + q)
+        srcs = [T.land1[4 * j + u] for j in range(8) if j != k] + [T.xd[4 * m + q]]
+        trs.append(RemoteDMATransfer(dst_ids=[dst(coll)], dma_engine_mask=((1 << ne) - 1) << (ne * u),
                                      remote_sem=sem.arr2, srcs=srcs, dsts=[T.land2[c - FIRST_CHIP]], alu_op=1))
     g.remote_dma_fused(trs, local_sem=sem.sent)
     sent += 4 * ne
 
-    g.wait_ge(sem.arr2, 2 + 2 + 2 + 4)
+    g.wait_ge(sem.arr2, 2 + 2 + 4 + 4)
     q = k % 4
     owners = [8 * c + (4 + t if k < 4 else t) for t in range(4)]
     g.remote_dma_fused([RemoteDMATransfer(dst_ids=[dst(o) for o in owners], dma_engine_mask=0xFFFF,

@@ -6,7 +6,7 @@ SCRATCH = {
     "land2": ("dram", [4, 128, 64], "bfloat16"),
     "grp": ("dram", [4, 128, 64], "bfloat16"),
 }
-SEMAPHORES = ["ldA", "ldB", "sent", "arr1", "arr2", "arr3", "stored"]
+SEMAPHORES = ["ldA", "ldB", "sent", "arr1", "arr1a", "arr1b", "arr2", "arr3", "stored"]
 
 FIRST_CHIP = 4
 
@@ -47,34 +47,41 @@ def rank_program(g, core, T, topo):
             qu = g.sync if i % 2 == 0 else g.scalar
             qu.dma_start(T.xd[4 * m:4 * m + 4], T.x[:, 256 * m:256 * m + 256]).then_inc(ld, 16)
 
+    port = k in (2, 3, 6, 7)
     sent = 0
-    for groups, ld in ((first, sem.ldA), (second, sem.ldB)):
+    for groups, qs, ld, ne, arr in ((first, (0, 1), sem.ldA, 2, sem.arr1a), (first, (2, 3), sem.ldA, 2, sem.arr1b),
+                                    (second, (0, 1, 2, 3), sem.ldB, 1, sem.arr1)):
         g.wait_ge(ld, 64)
         trs = []
         for m in groups:
-            for q in range(4):
+            for q in qs:
                 r = reducer_of(c, m, q)
                 if r == k:
                     continue
                 u = units_of(c, r).index((m, q))
-                trs.append(RemoteDMATransfer(dst_ids=[dst(8 * c + r)], dma_engine_mask=1 << len(trs),
-                                             remote_sem=sem.arr1, src=T.xd[4 * m + q], dst=T.land1[4 * k + u],
-                                             alu_op=0))
+                trs.append(RemoteDMATransfer(dst_ids=[dst(8 * c + r)],
+                                             dma_engine_mask=((1 << ne) - 1) << (ne * len(trs)),
+                                             remote_sem=arr, src=T.xd[4 * m + q], dst=T.land1[4 * k + u], alu_op=0))
         g.remote_dma_fused(trs, local_sem=sem.sent)
-        sent += len(trs)
+        sent += ne * len(trs)
 
-    g.wait_ge(sem.arr1, 28)
-    ne = 2 if k in (2, 3, 6, 7) else 4
-    trs = []
-    for u, (m, q) in enumerate(mine):
-        coll = 8 * (FIRST_CHIP + m // 2) + (q if m % 2 else 4 + q)
-        srcs = [T.land1[4 * j + u] for j in range(8) if j != k] + [T.xd[4 * m + q]]
-        trs.append(RemoteDMATransfer(dst_ids=[dst(coll)], dma_engine_mask=((1 << ne) - 1) << (ne * u),
-                                     remote_sem=sem.arr2, srcs=srcs, dsts=[T.land2[c - FIRST_CHIP]], alu_op=1))
-    g.remote_dma_fused(trs, local_sem=sem.sent)
-    sent += 4 * ne
+    if port:
+        calls = (((0, 1), sem.arr1a), ((2, 3), sem.arr1b))
+    else:
+        calls = (((0, 1, 2, 3), sem.arr1),)
+    for us, arr in calls:
+        g.wait_ge(arr, 28)
+        trs = []
+        for u in us:
+            m, q = mine[u]
+            coll = 8 * (FIRST_CHIP + m // 2) + (q if m % 2 else 4 + q)
+            srcs = [T.land1[4 * j + u] for j in range(8) if j != k] + [T.xd[4 * m + q]]
+            trs.append(RemoteDMATransfer(dst_ids=[dst(coll)], dma_engine_mask=0xF << (4 * len(trs)),
+                                         remote_sem=sem.arr2, srcs=srcs, dsts=[T.land2[c - FIRST_CHIP]], alu_op=1))
+        g.remote_dma_fused(trs, local_sem=sem.sent)
+        sent += 4 * len(trs)
 
-    g.wait_ge(sem.arr2, 2 + 2 + 4 + 4)
+    g.wait_ge(sem.arr2, 4 * 4)
     q = k % 4
     owners = [8 * c + (4 + t if k < 4 else t) for t in range(4)]
     g.remote_dma_fused([RemoteDMATransfer(dst_ids=[dst(o) for o in owners], dma_engine_mask=0xFFFF,

from concourse.bass import DstId, RemoteDMATransfer

SCRATCH = {
    "xd": ("dram", [32, 128, 64], "bfloat16"),
    "land1": ("dram", [32, 128, 64], "bfloat16"),
    "land2": ("dram", [4, 128, 64], "bfloat16"),
    "grp": ("dram", [4, 128, 64], "bfloat16"),
}
SEMAPHORES = ["ldA", "ldB", "sent", "arr1", "arr1a", "arr1b", "arr2", "arr3", "stored"]

FIRST_CHIP = 4


def reducer_of(c, m, q):
    cc, hi = FIRST_CHIP + m // 2, m % 2
    if cc == c:
        return (4 if hi else 0) + q // 2
    if cc == c ^ 2:
        return (0 if hi else 4) + q // 2
    if cc == c ^ 1:
        return 2 if hi else 6
    return 3 if hi else 7


def units_of(c, k):
    us = [(m, q) for m in range(8) for q in range(4) if reducer_of(c, m, q) == k]
    return sorted(us, key=lambda u: (FIRST_CHIP + u[0] // 2 == c, u))


def rank_program(g, core, T, topo):
    rank = T.rank_of(core)
    if rank is None:
        return
    c, k = topo.chip(core), core % 8
    sem = T.sem

    def dst(cr):
        rid, pid, _se = topo.addr(cr)
        return DstId(rid=rid, pnc=pid)

    mine = units_of(c, k)
    first = [m for m in range(8) if (FIRST_CHIP + m // 2 - c) % 2 == 1]
    second = [m for m in range(8) if m not in first]

    for groups, ld in ((first, sem.ldA), (second, sem.ldB)):
        for i, m in enumerate(groups):
            qu = g.sync if i % 2 == 0 else g.scalar
            qu.dma_start(T.xd[4 * m:4 * m + 4], T.x[:, 256 * m:256 * m + 256]).then_inc(ld, 16)

    port = k in (2, 3, 6, 7)
    sent = 0
    for groups, qs, ld, ne, arr in ((first, (0, 1), sem.ldA, 2, sem.arr1a), (first, (2, 3), sem.ldA, 2, sem.arr1b),
                                    (second, (0, 1, 2, 3), sem.ldB, 1, sem.arr1)):
        g.wait_ge(ld, 64)
        trs = []
        for m in groups:
            for q in qs:
                r = reducer_of(c, m, q)
                if r == k:
                    continue
                u = units_of(c, r).index((m, q))
                trs.append(RemoteDMATransfer(dst_ids=[dst(8 * c + r)],
                                             dma_engine_mask=((1 << ne) - 1) << (ne * len(trs)),
                                             remote_sem=arr, src=T.xd[4 * m + q], dst=T.land1[4 * k + u], alu_op=0))
        g.remote_dma_fused(trs, local_sem=sem.sent)
        sent += ne * len(trs)

    if port:
        calls = (((0, 1), sem.arr1a), ((2, 3), sem.arr1b))
    else:
        calls = (((0, 1, 2, 3), sem.arr1),)
    for us, arr in calls:
        g.wait_ge(arr, 28)
        trs = []
        for u in us:
            m, q = mine[u]
            coll = 8 * (FIRST_CHIP + m // 2) + (q if m % 2 else 4 + q)
            srcs = [T.land1[4 * j + u] for j in range(8) if j != k] + [T.xd[4 * m + q]]
            trs.append(RemoteDMATransfer(dst_ids=[dst(coll)], dma_engine_mask=0xF << (4 * len(trs)),
                                         remote_sem=sem.arr2, srcs=srcs, dsts=[T.land2[c - FIRST_CHIP]], alu_op=1))
        g.remote_dma_fused(trs, local_sem=sem.sent)
        sent += 4 * len(trs)

    g.wait_ge(sem.arr2, 4 * 4)
    q = k % 4
    owners = [8 * c + (4 + t if k < 4 else t) for t in range(4)]
    g.remote_dma_fused([RemoteDMATransfer(dst_ids=[dst(o) for o in owners], dma_engine_mask=0xFFFF,
                                          remote_sem=sem.arr3, srcs=[T.land2[i] for i in range(4)],
                                          dsts=[T.grp[q] for _o in owners], alu_op=1)], local_sem=sem.sent)
    sent += 16

    t = k % 4
    g.sync.wait_ge(sem.arr3, 64)
    g.sync.dma_start(T.y[:], T.grp[:, t::4, :]).then_inc(sem.stored, 16)

    g.wait_ge(sem.sent, sent)
    g.wait_ge(sem.stored, 16)
